import numpy as np
import ml_dtypes


def mxq(x, axis, fmt="e4m3"):
    dtype, down = {"e4m3": (ml_dtypes.float8_e4m3fn, 7), "e5m2": (ml_dtypes.float8_e5m2, 14)}[fmt]
    v = np.moveaxis(np.asarray(x, np.float32).astype(ml_dtypes.bfloat16).astype(np.float64), axis, -1)
    blocks = v.reshape(v.shape[:-1] + (-1, 32))
    amax = np.abs(blocks).max(-1, keepdims=True)
    byte = np.maximum(np.where(amax > 0, np.frexp(amax)[1] - 1 + 127, 0) - down, 1)
    scale = np.exp2(byte - 127.0)
    codes = (blocks / scale).astype(np.float32).astype(dtype).astype(np.float64)
    return np.moveaxis((codes * scale).reshape(v.shape), -1, axis)


WIDE = False


def mx_kscale(k):
    if not WIDE:
        return np.ones(k)
    levels = np.array([10, -10, 5, -5, 0])
    if k % 512:
        return np.exp2(np.random.permutation(np.resize(levels, k // 32))).repeat(32)
    a = np.empty((k // 512, 16))
    for p in range(k // 512):
        a[p, :8] = np.random.permutation(np.resize(levels, 8))
        for g in range(8):
            far = levels[np.abs(levels - a[p, g]) >= 10]
            a[p, g + 8] = far[np.random.randint(len(far))]
    return np.exp2(a.ravel()).repeat(32)


def f64(x):
    return np.asarray(x).astype(np.float64)


def striped(idx):
    return np.tile(idx.reshape(-1, 16).T, (8, 1)).astype(np.uint16)


def unstriped(offs):
    return offs[:16].T.reshape(-1).astype(np.int64)


E2M1 = np.array([0.0, 0.5, 1.0, 1.5, 2.0, 3.0, 4.0, 6.0, -0.0, -0.5, -1.0, -1.5, -2.0, -3.0, -4.0, -6.0])


def pack_weight(w, fmt):
    k, n = w.shape
    w = f64(np.asarray(w, np.float32).astype(ml_dtypes.bfloat16)).reshape(k // 32, 32, n)
    amax = np.abs(w).max(1)
    if fmt == "e4m3":
        byte = np.frexp(amax)[1] - 1 + 127 - 7
    else:
        mant, ex = np.frexp(amax / 6.0)
        byte = np.where(mant > 0.5, ex, ex - 1) + 127
    byte = np.clip(np.where(amax > 0, byte, 1), 1, 254)
    scaled = (w * np.exp2(127.0 - byte)[:, None, :]).reshape(k, n).astype(np.float32)
    by_word = np.ascontiguousarray(scaled.reshape(k // 512, 128, 4, n).transpose(0, 1, 3, 2))
    if fmt == "e4m3":
        words = by_word.astype(ml_dtypes.float8_e4m3fn).view(np.uint8)
    else:
        c = by_word.astype(ml_dtypes.float4_e2m1fn).view(np.uint8) & 0xF
        words = (c[..., 0::2] | (c[..., 1::2] << 4)).reshape(k // 512, 128, 2 * n)
    return np.ascontiguousarray(words), np.ascontiguousarray(byte.astype(np.uint8).reshape(k // 512, 16, n))


def unpack_weight(words, scales, fmt):
    g, _, n = scales.shape
    words = np.ascontiguousarray(words).reshape(g, 128, n, -1)
    if fmt == "e4m3":
        vals = words.view(ml_dtypes.float8_e4m3fn).astype(np.float64)
    else:
        nib = np.empty((g, 128, n, 4), np.uint8)
        nib[..., 0::2] = words & 0xF
        nib[..., 1::2] = words >> 4
        vals = E2M1[nib]
    vals = vals * np.repeat(np.exp2(scales.astype(np.float64) - 127.0), 8, axis=1)[..., None]
    return vals.transpose(0, 1, 3, 2).reshape(g * 512, n)


K, T, E, C, N = 2048, 768, 6, 128, 128


def by_expert(wq, xq):
    return np.concatenate([wq[e].T @ xq[:, e * C:(e + 1) * C] for e in range(E)], axis=1)


def setup_inputs():
    n = np.random.standard_normal
    s = mx_kscale(K)[:, None]
    w = [pack_weight(m, "e2m1") for m in n((E, K, N)) / np.sqrt(K) / s[None]]
    return {
        "xT": (n((K, T)) * s).astype(np.float32),
        "w_words": np.stack([m[0] for m in w]),
        "w_scales": np.stack([m[1] for m in w]),
        "b": (0.3 * n((N, E))).astype(np.float32),
        "gate": np.tile(np.random.uniform(0.2, 1.0, E * C), (K, 1)).astype(np.float32),
        "offs": striped(np.random.permutation(T)[:E * C]),
    }


def reference(xT, w_words, w_scales, b, gate, offs):
    idx = unstriped(offs)
    w = np.stack([unpack_weight(w_words[e], w_scales[e], "e2m1") for e in range(E)])
    xq = mxq(f64(gate) * f64(xT)[:, idx], 0, "e4m3")
    y = by_expert(w, xq)
    y = y + np.repeat(f64(b), C, axis=1)
    out = np.zeros((N, T))
    out[:, idx] = y
    return out

@@ -1,0 +1,159 @@
+from contextlib import ExitStack
+
+import concourse.mybir as mybir
+from concourse.masks import make_identity
+
+K, T, E, C, N = 2048, 768, 6, 128, 128
+
+F32 = mybir.dt.float32
+BF16 = mybir.dt.bfloat16
+I32 = mybir.dt.int32
+U32 = mybir.dt.uint32
+U16 = mybir.dt.uint16
+U8 = mybir.dt.uint8
+FP8X4 = mybir.dt.float8_e4m3fn_x4
+FP4X4 = mybir.dt.float4_e2m1fn_x4
+COPY = mybir.ActivationFunctionType.Copy
+IDENTITY = mybir.ActivationFunctionType.Identity
+
+P = 128
+PACK = 4
+PASSES = K // (P * PACK)
+PAIR = 2 * C
+PAIRS = E // 2
+WIDE = 1024
+PER_COLUMN = 16
+
+FLOPS = 2 * K * N * E * C
+BYTES = 4 * K * T + E * K * N // 2 + E * K * N // 32 + 4 * N * E + 4 * T + 2 * P * T // PER_COLUMN + 4 * N * T
+
+
+def tile_moe_pre_lin_bias_kernel(tc, xT, w_words, w_scales, b, gate, offs, out):
+    nc = tc.nc
+    last = PASSES - 1
+    with ExitStack() as ctx:
+        keep = ctx.enter_context(tc.tile_pool(name="keep", bufs=1))
+        ring = ctx.enter_context(tc.tile_pool(name="ring", bufs=4))
+        turn_in = ctx.enter_context(tc.psum_pool(name="turn_in", bufs=3))
+        turn_back = ctx.enter_context(tc.psum_pool(name="turn_back", bufs=2))
+        sums = ctx.enter_context(tc.psum_pool(name="sums", bufs=3))
+
+        offsets = keep.tile([P, T // PER_COLUMN], U16, name="offsets")
+        nc.sync.dma_start(offsets[:], offs)
+
+        planes = PASSES * PACK
+        tokens = keep.tile([P, planes * T + WIDE - T], F32, name="tokens")
+        nc.vector.memset(tokens[:, planes * T :], 0.0)
+        rows = xT.rearrange("(a p t) w -> a p t w", p=P, t=PACK)
+
+        def column_of(a, t):
+            if a == last:
+                return t * T
+            return (planes - 1 - (a * PACK + t)) * T
+
+        def load_plane(a, t):
+            first = column_of(a, t)
+            nc.sync.dma_start(out=tokens[:, first : first + T], in_=rows[a, :, t, :])
+
+        for a in range(last):
+            for t in range(PACK):
+                load_plane(a, t)
+
+        groups = E * PASSES
+        w_codes = keep.tile([P, groups * 2 * N], U8, name="w_codes", align_bytes=64)
+        nc.sync.dma_start(
+            out=w_codes[:].bitcast(I32).rearrange("p (g n) -> p g n", g=groups),
+            in_=w_words.rearrange("e a p n -> p (e a) n").bitcast(I32),
+        )
+        w_plane = keep.tile([P, groups * N], U8, name="w_plane", align_bytes=64)
+        w_plane_words = w_plane[:].bitcast(I32)
+        nc.gpsimd.memset(w_plane_words, 0)
+        scale_rows = w_scales.rearrange("e a (q r) n -> r q (e a) n", r=4).bitcast(I32)
+        for r in range(4):
+            nc.sync.dma_start(
+                out=w_plane_words[r:P:32, :].rearrange("q (g n) -> q g n", g=groups),
+                in_=scale_rows[r],
+            )
+        nc.sync.dma_start(
+            out=tokens[:, 0 : PACK * T].rearrange("p (t w) -> p t w", t=PACK),
+            in_=rows[last],
+        )
+
+        identity = keep.tile([P, P], F32, name="identity")
+        make_identity(nc, identity[:])
+        bias = keep.tile([P, E], F32, name="bias")
+        nc.scalar.dma_start(out=bias[:], in_=b)
+        gate_rows = keep.tile([P, C], F32, name="gate_rows")
+        nc.vector.memset(gate_rows[:], 0.0)
+        nc.scalar.dma_start(out=gate_rows[0:E, :], in_=gate[0].rearrange("(e c) -> e c", e=E))
+        gate_turned = turn_in.tile([P, PACK * P], F32, name="by_slot")
+        nc.tensor.transpose(gate_turned[:, 0:P], gate_rows[:], identity[:])
+        gate_of_slot = keep.tile([P, E], F32, name="gate_of_slot")
+        nc.scalar.copy(out=gate_of_slot[:], in_=gate_turned[:, 0:E])
+
+        x_codes = {}
+        x_planes = {}
+
+        def quantise_pair(a, pair, gathered, first):
+            back = turn_back.tile([P, 2 * PAIR], F32, name="back")
+            for j in range(2):
+                e = 2 * pair + j
+                slots = slice(first + j * C, first + (j + 1) * C)
+                by_slot = turn_in.tile([P, PACK * P], F32, name="by_slot")
+                for t in range(PACK):
+                    nc.tensor.transpose(by_slot[:, t * P : (t + 1) * P], gathered[:, t, slots], identity[:])
+                gated = ring.tile([P, PACK * P], BF16, name="gated")
+                nc.scalar.activation(
+                    out=gated[:].rearrange("s (u p h) -> s u p h", u=2, h=2),
+                    in_=by_slot[:].rearrange("s (u h p) -> s u p h", u=2, h=2),
+                    func=COPY,
+                    scale=gate_of_slot[:, e : e + 1],
+                )
+                words = gated[:].bitcast(F32)
+                for u in range(2):
+                    at = (2 * j + u) * P
+                    nc.tensor.transpose(back[:, at : at + P], words[:, u * P : (u + 1) * P], identity[:])
+            grouped = ring.tile([P, PACK * PAIR], BF16, name="grouped", align_bytes=64)
+            nc.scalar.copy(
+                out=grouped[:].bitcast(F32).rearrange("p (j s u) -> p j s u", j=2, u=2),
+                in_=back[:].rearrange("p (j u s) -> p j s u", j=2, u=2),
+            )
+            x_codes[a, pair] = keep.tile([P, PAIR], U32, name="x_codes_%d_%d" % (a, pair), align_bytes=64)
+            x_planes[a, pair] = keep.tile([P, PAIR], U8, name="x_plane_%d_%d" % (a, pair), align_bytes=64)
+            nc.vector.quantize_mx(out=x_codes[a, pair][:].bitcast(FP8X4), scales=x_planes[a, pair][:], in_=grouped[:])
+
+        for a in range(last):
+            gathered = keep.tile([P, PACK, T], F32, name="gathered_%d" % a)
+            for t in range(PACK):
+                first = column_of(a, t)
+                nc.vector.tensor_copy(gathered[:, t, :], tokens[:, first : first + WIDE].indirect(offsets[:]))
+            for pair in range(PAIRS):
+                quantise_pair(a, pair, gathered, pair * PAIR)
+
+        result = keep.tile([P, T], F32, name="result")
+        for pair in range(PAIRS):
+            pair_offsets = offsets[:, pair * PAIR // PER_COLUMN : (pair + 1) * PAIR // PER_COLUMN]
+            gathered = keep.tile([P, PACK, PAIR], F32, name="gathered_last_%d" % pair)
+            for t in range(PACK):
+                first = column_of(last, t)
+                nc.vector.tensor_copy(gathered[:, t, :], tokens[:, first : first + T].indirect(pair_offsets))
+            quantise_pair(last, pair, gathered, 0)
+            by_expert = keep.tile([P, PAIR], F32, name="by_expert_%d" % pair)
+            for j in range(2):
+                e = 2 * pair + j
+                slots = slice(j * C, (j + 1) * C)
+                acc = sums.tile([P, C], F32, name="acc")
+                for a in range(PASSES):
+                    g = e * PASSES + a
+                    nc.tensor.matmul_mx(
+                        out=acc[:],
+                        lhsT=w_codes[:, g * 2 * N : (g + 1) * 2 * N].bitcast(FP4X4),
+                        lhsT_scale=w_plane[:, g * N : (g + 1) * N],
+                        rhs=x_codes[a, pair][:, slots].bitcast(FP8X4),
+                        rhs_scale=x_planes[a, pair][:, slots],
+                        start=(a == 0),
+                        stop=(a == last),
+                    )
+                nc.scalar.activation(out=by_expert[:, slots], in_=acc[:], func=IDENTITY, bias=bias[:, e : e + 1])
+            nc.vector.tensor_copy(result[:].indirect(pair_offsets), by_expert[:])
+        nc.sync.dma_start(out=out, in_=result[:])

@@ -1,7 +1,6 @@
 from contextlib import ExitStack
 
 import concourse.mybir as mybir
-from concourse.masks import make_identity
 
 K, T, E, C, N = 2048, 768, 6, 128, 128
 
@@ -13,7 +12,6 @@ U16 = mybir.dt.uint16
 U8 = mybir.dt.uint8
 FP8X4 = mybir.dt.float8_e4m3fn_x4
 FP4X4 = mybir.dt.float4_e2m1fn_x4
-COPY = mybir.ActivationFunctionType.Copy
 IDENTITY = mybir.ActivationFunctionType.Identity
 
 P = 128
@@ -21,7 +19,6 @@ PACK = 4
 PASSES = K // (P * PACK)
 PAIR = 2 * C
 PAIRS = E // 2
-WIDE = 1024
 PER_COLUMN = 16
 
 FLOPS = 2 * K * N * E * C
@@ -33,31 +30,22 @@ def tile_moe_pre_lin_bias_kernel(tc, xT, w_words, w_scales, b, gate, offs, out):
     last = PASSES - 1
     with ExitStack() as ctx:
         keep = ctx.enter_context(tc.tile_pool(name="keep", bufs=1))
-        ring = ctx.enter_context(tc.tile_pool(name="ring", bufs=4))
-        turn_in = ctx.enter_context(tc.psum_pool(name="turn_in", bufs=3))
-        turn_back = ctx.enter_context(tc.psum_pool(name="turn_back", bufs=2))
-        sums = ctx.enter_context(tc.psum_pool(name="sums", bufs=3))
+        sums = ctx.enter_context(tc.psum_pool(name="sums", bufs=6))
 
         offsets = keep.tile([P, T // PER_COLUMN], U16, name="offsets")
-        nc.sync.dma_start(offsets[:], offs)
 
-        planes = PASSES * PACK
-        tokens = keep.tile([P, planes * T + WIDE - T], F32, name="tokens")
-        nc.vector.memset(tokens[:, planes * T :], 0.0)
         rows = xT.rearrange("(a p t) w -> a p t w", p=P, t=PACK)
-
-        def column_of(a, t):
-            if a == last:
-                return t * T
-            return (planes - 1 - (a * PACK + t)) * T
-
-        def load_plane(a, t):
-            first = column_of(a, t)
-            nc.sync.dma_start(out=tokens[:, first : first + T], in_=rows[a, :, t, :])
-
-        for a in range(last):
+        window = {}
+        gates = []
+        for a in range(PASSES):
             for t in range(PACK):
-                load_plane(a, t)
+                window[a, t] = keep.tile([P, T], F32, name="tokens_%d_%d" % (a, t))
+                nc.sync.dma_start(out=window[a, t][:], in_=rows[a, :, t, :])
+                if (a, t) == (0, 0):
+                    nc.sync.dma_start(offsets[:], offs)
+                if a == 0 and t < PAIRS:
+                    gates.append(keep.tile([P, PAIR], F32, name="gate_%d" % t))
+                    nc.sync.dma_start(out=gates[t][:], in_=gate[0:P, t * PAIR : (t + 1) * PAIR])
 
         groups = E * PASSES
         w_codes = keep.tile([P, groups * 2 * N], U8, name="w_codes", align_bytes=64)
@@ -74,76 +62,46 @@ def tile_moe_pre_lin_bias_kernel(tc, xT, w_words, w_scales, b, gate, offs, out):
                 out=w_plane_words[r:P:32, :].rearrange("q (g n) -> q g n", g=groups),
                 in_=scale_rows[r],
             )
-        nc.sync.dma_start(
-            out=tokens[:, 0 : PACK * T].rearrange("p (t w) -> p t w", t=PACK),
-            in_=rows[last],
-        )
 
-        identity = keep.tile([P, P], F32, name="identity")
-        make_identity(nc, identity[:])
         bias = keep.tile([P, E], F32, name="bias")
-        nc.scalar.dma_start(out=bias[:], in_=b)
-        gate_rows = keep.tile([P, C], F32, name="gate_rows")
-        nc.vector.memset(gate_rows[:], 0.0)
-        nc.scalar.dma_start(out=gate_rows[0:E, :], in_=gate[0].rearrange("(e c) -> e c", e=E))
-        gate_turned = turn_in.tile([P, PACK * P], F32, name="by_slot")
-        nc.tensor.transpose(gate_turned[:, 0:P], gate_rows[:], identity[:])
-        gate_of_slot = keep.tile([P, E], F32, name="gate_of_slot")
-        nc.scalar.copy(out=gate_of_slot[:], in_=gate_turned[:, 0:E])
+        nc.sync.dma_start(out=bias[:], in_=b)
 
         x_codes = {}
         x_planes = {}
 
-        def quantise_pair(a, pair, gathered, first):
-            back = turn_back.tile([P, 2 * PAIR], F32, name="back")
-            for j in range(2):
-                e = 2 * pair + j
-                slots = slice(first + j * C, first + (j + 1) * C)
-                by_slot = turn_in.tile([P, PACK * P], F32, name="by_slot")
-                for t in range(PACK):
-                    nc.tensor.transpose(by_slot[:, t * P : (t + 1) * P], gathered[:, t, slots], identity[:])
-                gated = ring.tile([P, PACK * P], BF16, name="gated")
-                nc.scalar.activation(
-                    out=gated[:].rearrange("s (u p h) -> s u p h", u=2, h=2),
-                    in_=by_slot[:].rearrange("s (u h p) -> s u p h", u=2, h=2),
-                    func=COPY,
-                    scale=gate_of_slot[:, e : e + 1],
-                )
-                words = gated[:].bitcast(F32)
-                for u in range(2):
-                    at = (2 * j + u) * P
-                    nc.tensor.transpose(back[:, at : at + P], words[:, u * P : (u + 1) * P], identity[:])
-            grouped = ring.tile([P, PACK * PAIR], BF16, name="grouped", align_bytes=64)
+        def offsets_of(first, count):
+            return offsets[:, first // PER_COLUMN : (first + count) // PER_COLUMN]
+
+        def quantise_pair(a, pair):
+            gated = keep.tile([P, PACK, PAIR], F32, tag="gated_%d_%d" % (a, pair), name="gated")
+            for t in range(PACK):
+                looked_up = window[a, t][:].indirect(offsets_of(pair * PAIR, PAIR))
+                nc.vector.tensor_tensor(gated[:, t, :], looked_up, gates[pair][:], mybir.AluOpType.mult)
+            grouped = keep.tile([P, PACK * PAIR], BF16, tag="grouped_%d_%d" % (a, pair), name="grouped", align_bytes=64)
             nc.scalar.copy(
-                out=grouped[:].bitcast(F32).rearrange("p (j s u) -> p j s u", j=2, u=2),
-                in_=back[:].rearrange("p (j u s) -> p j s u", j=2, u=2),
+                out=grouped[:].rearrange("p (c i t) -> p c t i", i=4, t=PACK),
+                in_=gated[:].rearrange("p t (c i) -> p c t i", i=4),
             )
             x_codes[a, pair] = keep.tile([P, PAIR], U32, name="x_codes_%d_%d" % (a, pair), align_bytes=64)
             x_planes[a, pair] = keep.tile([P, PAIR], U8, name="x_plane_%d_%d" % (a, pair), align_bytes=64)
             nc.vector.quantize_mx(out=x_codes[a, pair][:].bitcast(FP8X4), scales=x_planes[a, pair][:], in_=grouped[:])
 
         for a in range(last):
-            gathered = keep.tile([P, PACK, T], F32, name="gathered_%d" % a)
-            for t in range(PACK):
-                first = column_of(a, t)
-                nc.vector.tensor_copy(gathered[:, t, :], tokens[:, first : first + WIDE].indirect(offsets[:]))
             for pair in range(PAIRS):
-                quantise_pair(a, pair, gathered, pair * PAIR)
+                quantise_pair(a, pair)
 
-        result = keep.tile([P, T], F32, name="result")
-        for pair in range(PAIRS):
-            pair_offsets = offsets[:, pair * PAIR // PER_COLUMN : (pair + 1) * PAIR // PER_COLUMN]
-            gathered = keep.tile([P, PACK, PAIR], F32, name="gathered_last_%d" % pair)
-            for t in range(PACK):
-                first = column_of(last, t)
-                nc.vector.tensor_copy(gathered[:, t, :], tokens[:, first : first + T].indirect(pair_offsets))
-            quantise_pair(last, pair, gathered, 0)
-            by_expert = keep.tile([P, PAIR], F32, name="by_expert_%d" % pair)
+        results = []
+
+        pass_order = [last] + list(range(last))
+
+        def finish(pair):
+            tag = "gated_%d_2" % last if pair == 1 else "by_expert_%d" % pair
+            by_expert = keep.tile([P, PAIR], F32, tag=tag, name="by_expert")
             for j in range(2):
                 e = 2 * pair + j
                 slots = slice(j * C, (j + 1) * C)
                 acc = sums.tile([P, C], F32, name="acc")
-                for a in range(PASSES):
+                for a in pass_order:
                     g = e * PASSES + a
                     nc.tensor.matmul_mx(
                         out=acc[:],
@@ -151,9 +109,17 @@ def tile_moe_pre_lin_bias_kernel(tc, xT, w_words, w_scales, b, gate, offs, out):
                         lhsT_scale=w_plane[:, g * N : (g + 1) * N],
                         rhs=x_codes[a, pair][:, slots].bitcast(FP8X4),
                         rhs_scale=x_planes[a, pair][:, slots],
-                        start=(a == 0),
-                        stop=(a == last),
+                        start=(a == pass_order[0]),
+                        stop=(a == pass_order[-1]),
                     )
                 nc.scalar.activation(out=by_expert[:, slots], in_=acc[:], func=IDENTITY, bias=bias[:, e : e + 1])
-            nc.vector.tensor_copy(result[:].indirect(pair_offsets), by_expert[:])
-        nc.sync.dma_start(out=out, in_=result[:])
+            if pair == 0:
+                results.append(keep.tile([P, T], F32, tag="grouped_%d_1" % last, name="result", align_bytes=64))
+            nc.vector.tensor_copy(results[0][:].indirect(offsets_of(pair * PAIR, PAIR)), by_expert[:])
+
+        for pair in range(PAIRS):
+            quantise_pair(last, pair)
+            if pair > 0:
+                finish(pair - 1)
+        finish(PAIRS - 1)
+        nc.sync.dma_start(out=out, in_=results[0][:])

@@ -13,13 +13,17 @@ U8 = mybir.dt.uint8
 FP8X4 = mybir.dt.float8_e4m3fn_x4
 FP4X4 = mybir.dt.float4_e2m1fn_x4
 IDENTITY = mybir.ActivationFunctionType.Identity
+MULT = mybir.AluOpType.mult
 
 P = 128
 PACK = 4
 PASSES = K // (P * PACK)
+LAST = PASSES - 1
 PAIR = 2 * C
 PAIRS = E // 2
 PER_COLUMN = 16
+SPARE = 16
+LINE = 4
 
 FLOPS = 2 * K * N * E * C
 BYTES = 4 * K * T + E * K * N // 2 + E * K * N // 32 + 4 * N * E + 4 * T + 2 * P * T // PER_COLUMN + 4 * N * T
@@ -27,99 +31,119 @@ BYTES = 4 * K * T + E * K * N // 2 + E * K * N // 32 + 4 * N * E + 4 * T + 2 * P
 
 def tile_moe_pre_lin_bias_kernel(tc, xT, w_words, w_scales, b, gate, offs, out):
     nc = tc.nc
-    last = PASSES - 1
     with ExitStack() as ctx:
         keep = ctx.enter_context(tc.tile_pool(name="keep", bufs=1))
-        sums = ctx.enter_context(tc.psum_pool(name="sums", bufs=6))
+        sums = ctx.enter_context(tc.psum_pool(name="sums", bufs=E))
 
-        offsets = keep.tile([P, T // PER_COLUMN], U16, name="offsets")
-
-        rows = xT.rearrange("(a p t) w -> a p t w", p=P, t=PACK)
-        window = {}
-        gates = []
-        for a in range(PASSES):
-            for t in range(PACK):
-                window[a, t] = keep.tile([P, T], F32, name="tokens_%d_%d" % (a, t))
-                nc.sync.dma_start(out=window[a, t][:], in_=rows[a, :, t, :])
-                if (a, t) == (0, 0):
-                    nc.sync.dma_start(offsets[:], offs)
-                if a == 0 and t < PAIRS:
-                    gates.append(keep.tile([P, PAIR], F32, name="gate_%d" % t))
-                    nc.sync.dma_start(out=gates[t][:], in_=gate[0:P, t * PAIR : (t + 1) * PAIR])
+        def by_pairs(a, t):
+            return a == LAST or (a, t) == (0, 0)
 
         groups = E * PASSES
         w_codes = keep.tile([P, groups * 2 * N], U8, name="w_codes", align_bytes=64)
-        nc.sync.dma_start(
-            out=w_codes[:].bitcast(I32).rearrange("p (g n) -> p g n", g=groups),
-            in_=w_words.rearrange("e a p n -> p (e a) n").bitcast(I32),
-        )
         w_plane = keep.tile([P, groups * N], U8, name="w_plane", align_bytes=64)
-        w_plane_words = w_plane[:].bitcast(I32)
-        nc.gpsimd.memset(w_plane_words, 0)
-        scale_rows = w_scales.rearrange("e a (q r) n -> r q (e a) n", r=4).bitcast(I32)
-        for r in range(4):
-            nc.sync.dma_start(
-                out=w_plane_words[r:P:32, :].rearrange("q (g n) -> q g n", g=groups),
-                in_=scale_rows[r],
-            )
-
         bias = keep.tile([P, E], F32, name="bias")
-        nc.sync.dma_start(out=bias[:], in_=b)
 
-        x_codes = {}
-        x_planes = {}
+        def load_weights():
+            nc.sync.dma_start(
+                out=w_codes[:].bitcast(I32).rearrange("p (g n) -> p g n", g=groups),
+                in_=w_words.rearrange("e a p n -> p (e a) n").bitcast(I32),
+            )
+            w_plane_words = w_plane[:].bitcast(I32)
+            nc.gpsimd.memset(w_plane_words, 0)
+            scale_rows = w_scales.rearrange("e a (q r) n -> r q (e a) n", r=4).bitcast(I32)
+            for r in range(4):
+                nc.sync.dma_start(
+                    out=w_plane_words[r:P:32, :].rearrange("q (g n) -> q g n", g=groups),
+                    in_=scale_rows[r],
+                )
+            nc.sync.dma_start(out=bias[:], in_=b)
+
+        offsets = keep.tile([P, T // PER_COLUMN], U16, name="offsets")
+        gates = keep.tile([P, T], F32, name="gates")
+        rows = xT.rearrange("(a p t) w -> a p t w", p=P, t=PACK)
+        window = {}
+        for a in range(PASSES):
+            for t in range(PACK):
+                width = T if by_pairs(a, t) else T + SPARE
+                window[a, t] = keep.tile([P, width], F32, name="tokens_%d_%d" % (a, t))
+                nc.sync.dma_start(out=window[a, t][:, 0:T], in_=rows[a, :, t, :])
+                if width > T:
+                    nc.gpsimd.memset(window[a, t][:, T:], 0.0)
+                if (a, t) == (0, 0):
+                    nc.sync.dma_start(offsets[:], offs)
+                    for pair in range(PAIRS):
+                        slots = slice(pair * PAIR, (pair + 1) * PAIR)
+                        nc.sync.dma_start(out=gates[:, slots], in_=gate[0:P, slots])
+                if (a, t) == (LAST - 1, PACK - 2):
+                    load_weights()
 
         def offsets_of(first, count):
             return offsets[:, first // PER_COLUMN : (first + count) // PER_COLUMN]
 
-        def quantise_pair(a, pair):
-            gated = keep.tile([P, PACK, PAIR], F32, tag="gated_%d_%d" % (a, pair), name="gated")
-            for t in range(PACK):
-                looked_up = window[a, t][:].indirect(offsets_of(pair * PAIR, PAIR))
-                nc.vector.tensor_tensor(gated[:, t, :], looked_up, gates[pair][:], mybir.AluOpType.mult)
-            grouped = keep.tile([P, PACK * PAIR], BF16, tag="grouped_%d_%d" % (a, pair), name="grouped", align_bytes=64)
+        def gather(into, a, t, first, count):
+            looked_up = window[a, t][:].indirect(offsets_of(first, count))
+            nc.vector.tensor_tensor(into, looked_up, gates[:, first : first + count], MULT)
+
+        x_codes = {}
+        x_planes = {}
+
+        def quantise(gated, a, first, count, tag):
+            grouped = keep.tile([P, PACK * count], BF16, tag=tag, name="grouped", align_bytes=64)
             nc.scalar.copy(
-                out=grouped[:].rearrange("p (c i t) -> p c t i", i=4, t=PACK),
-                in_=gated[:].rearrange("p t (c i) -> p c t i", i=4),
+                out=grouped[:].rearrange("p (c i t) -> p c t i", i=LINE, t=PACK),
+                in_=gated.rearrange("p t (c i) -> p c t i", i=LINE),
             )
-            x_codes[a, pair] = keep.tile([P, PAIR], U32, name="x_codes_%d_%d" % (a, pair), align_bytes=64)
-            x_planes[a, pair] = keep.tile([P, PAIR], U8, name="x_plane_%d_%d" % (a, pair), align_bytes=64)
-            nc.vector.quantize_mx(out=x_codes[a, pair][:].bitcast(FP8X4), scales=x_planes[a, pair][:], in_=grouped[:])
+            codes = keep.tile([P, count], U32, name="x_codes_%d_%d" % (a, first), align_bytes=64)
+            plane = keep.tile([P, count], U8, name="x_plane_%d_%d" % (a, first), align_bytes=64)
+            nc.vector.quantize_mx(out=codes[:].bitcast(FP8X4), scales=plane[:], in_=grouped[:])
+            for at in range(0, count, C):
+                x_codes[a, (first + at) // C] = codes[:, at : at + C]
+                x_planes[a, (first + at) // C] = plane[:, at : at + C]
 
-        for a in range(last):
-            for pair in range(PAIRS):
-                quantise_pair(a, pair)
+        for a in range(LAST):
+            gated = keep.tile([P, PACK, T], F32, name="gated_%d" % a)
+            for t in range(PACK):
+                count = PAIR if by_pairs(a, t) else T
+                for first in range(0, T, count):
+                    gather(gated[:, t, first : first + count], a, t, first, count)
+            for first, count in ((0, 2 * PAIR), (2 * PAIR, PAIR)):
+                quantise(gated[:, :, first : first + count], a, first, count, "grouped_%d_%d" % (a, first))
 
-        results = []
+        def last_pass(pair):
+            tag = "last_grouped_0" if pair == 2 else "last_gated_%d" % pair
+            gated = keep.tile([P, PACK, PAIR], F32, tag=tag, name="gated", align_bytes=64)
+            for t in range(PACK):
+                gather(gated[:, t, :], LAST, t, pair * PAIR, PAIR)
+            quantise(gated[:], LAST, pair * PAIR, PAIR, "last_grouped_%d" % pair if pair < 2 else "grouped_end")
 
-        pass_order = [last] + list(range(last))
-
-        def finish(pair):
-            tag = "gated_%d_2" % last if pair == 1 else "by_expert_%d" % pair
-            by_expert = keep.tile([P, PAIR], F32, tag=tag, name="by_expert")
+        def products(pair):
+            tag = "last_grouped_0" if pair == 1 else "by_expert_%d" % pair
+            by_expert = keep.tile([P, PAIR], F32, tag=tag, name="by_expert", align_bytes=64)
             for j in range(2):
                 e = 2 * pair + j
-                slots = slice(j * C, (j + 1) * C)
                 acc = sums.tile([P, C], F32, name="acc")
-                for a in pass_order:
+                for a in range(PASSES):
                     g = e * PASSES + a
                     nc.tensor.matmul_mx(
                         out=acc[:],
                         lhsT=w_codes[:, g * 2 * N : (g + 1) * 2 * N].bitcast(FP4X4),
                         lhsT_scale=w_plane[:, g * N : (g + 1) * N],
-                        rhs=x_codes[a, pair][:, slots].bitcast(FP8X4),
-                        rhs_scale=x_planes[a, pair][:, slots],
-                        start=(a == pass_order[0]),
-                        stop=(a == pass_order[-1]),
+                        rhs=x_codes[a, e].bitcast(FP8X4),
+                        rhs_scale=x_planes[a, e],
+                        start=(a == 0),
+                        stop=(a == LAST),
                     )
-                nc.scalar.activation(out=by_expert[:, slots], in_=acc[:], func=IDENTITY, bias=bias[:, e : e + 1])
-            if pair == 0:
-                results.append(keep.tile([P, T], F32, tag="grouped_%d_1" % last, name="result", align_bytes=64))
-            nc.vector.tensor_copy(results[0][:].indirect(offsets_of(pair * PAIR, PAIR)), by_expert[:])
+                nc.scalar.activation(
+                    out=by_expert[:, j * C : (j + 1) * C], in_=acc[:], func=IDENTITY, bias=bias[:, e : e + 1]
+                )
+            return by_expert
 
+        last_pass(0)
+        last_pass(1)
+        ready = [products(0)]
+        last_pass(2)
+        ready += [products(1), products(2)]
+        result = keep.tile([P, T], F32, tag="last_grouped_1", name="result", align_bytes=64)
         for pair in range(PAIRS):
-            quantise_pair(last, pair)
-            if pair > 0:
-                finish(pair - 1)
-        finish(PAIRS - 1)
-        nc.sync.dma_start(out=out, in_=results[0][:])
+            nc.vector.tensor_copy(result[:].indirect(offsets_of(pair * PAIR, PAIR)), ready[pair][:])
+        nc.sync.dma_start(out=out, in_=result[:])

@@ -24,6 +24,9 @@ PAIRS = E // 2
 PER_COLUMN = 16
 SPARE = 16
 LINE = 4
+QUADRANT = 32
+SCALE_ROWS = 4
+ALIGN = 64
 
 FLOPS = 2 * K * N * E * C
 BYTES = 4 * K * T + E * K * N // 2 + E * K * N // 32 + 4 * N * E + 4 * T + 2 * P * T // PER_COLUMN + 4 * N * T
@@ -38,22 +41,22 @@ def tile_moe_pre_lin_bias_kernel(tc, xT, w_words, w_scales, b, gate, offs, out):
         def by_pairs(a, t):
             return a == LAST or (a, t) == (0, 0)
 
-        groups = E * PASSES
-        w_codes = keep.tile([P, groups * 2 * N], U8, name="w_codes", align_bytes=64)
-        w_plane = keep.tile([P, groups * N], U8, name="w_plane", align_bytes=64)
+        matrices = E * PASSES
+        w_codes = keep.tile([P, matrices * 2 * N], U8, name="w_codes", align_bytes=ALIGN)
+        w_bytes = keep.tile([P, matrices * N], U8, name="w_bytes", align_bytes=ALIGN)
         bias = keep.tile([P, E], F32, name="bias")
 
         def load_weights():
             nc.sync.dma_start(
-                out=w_codes[:].bitcast(I32).rearrange("p (g n) -> p g n", g=groups),
+                out=w_codes[:].bitcast(I32).rearrange("p (g n) -> p g n", g=matrices),
                 in_=w_words.rearrange("e a p n -> p (e a) n").bitcast(I32),
             )
-            w_plane_words = w_plane[:].bitcast(I32)
-            nc.gpsimd.memset(w_plane_words, 0)
-            scale_rows = w_scales.rearrange("e a (q r) n -> r q (e a) n", r=4).bitcast(I32)
-            for r in range(4):
+            w_bytes_raw = w_bytes[:].bitcast(I32)
+            nc.gpsimd.memset(w_bytes_raw, 0)
+            scale_rows = w_scales.rearrange("e a (q r) n -> r q (e a) n", r=SCALE_ROWS).bitcast(I32)
+            for r in range(SCALE_ROWS):
                 nc.sync.dma_start(
-                    out=w_plane_words[r:P:32, :].rearrange("q (g n) -> q g n", g=groups),
+                    out=w_bytes_raw[r:P:QUADRANT, :].rearrange("q (g n) -> q g n", g=matrices),
                     in_=scale_rows[r],
                 )
             nc.sync.dma_start(out=bias[:], in_=b)
@@ -62,20 +65,26 @@ def tile_moe_pre_lin_bias_kernel(tc, xT, w_words, w_scales, b, gate, offs, out):
         gates = keep.tile([P, T], F32, name="gates")
         rows = xT.rearrange("(a p t) w -> a p t w", p=P, t=PACK)
         window = {}
-        for a in range(PASSES):
-            for t in range(PACK):
-                width = T if by_pairs(a, t) else T + SPARE
-                window[a, t] = keep.tile([P, width], F32, name="tokens_%d_%d" % (a, t))
-                nc.sync.dma_start(out=window[a, t][:, 0:T], in_=rows[a, :, t, :])
-                if width > T:
-                    nc.gpsimd.memset(window[a, t][:, T:], 0.0)
-                if (a, t) == (0, 0):
-                    nc.sync.dma_start(offsets[:], offs)
-                    for pair in range(PAIRS):
-                        slots = slice(pair * PAIR, (pair + 1) * PAIR)
-                        nc.sync.dma_start(out=gates[:, slots], in_=gate[0:P, slots])
-                if (a, t) == (LAST - 1, PACK - 2):
-                    load_weights()
+
+        def load_plane(a, t):
+            width = T if by_pairs(a, t) else T + SPARE
+            window[a, t] = keep.tile([P, width], F32, tag="tokens_%d_%d" % (a, t), name="tokens", align_bytes=ALIGN)
+            nc.sync.dma_start(out=window[a, t][:, 0:T], in_=rows[a, :, t, :])
+            if width > T:
+                nc.gpsimd.memset(window[a, t][:, T:], 0.0)
+
+        load_plane(0, 0)
+        nc.sync.dma_start(offsets[:], offs)
+        for pair in range(PAIRS):
+            slots = slice(pair * PAIR, (pair + 1) * PAIR)
+            nc.sync.dma_start(out=gates[:, slots], in_=gate[0:P, slots])
+        early = [(a, t) for a in range(LAST) for t in range(PACK)]
+        for a, t in early[1:-1]:
+            load_plane(a, t)
+        load_weights()
+        for t in range(PACK):
+            load_plane(LAST, t)
+        load_plane(*early[-1])
 
         def offsets_of(first, count):
             return offsets[:, first // PER_COLUMN : (first + count) // PER_COLUMN]
@@ -85,20 +94,20 @@ def tile_moe_pre_lin_bias_kernel(tc, xT, w_words, w_scales, b, gate, offs, out):
             nc.vector.tensor_tensor(into, looked_up, gates[:, first : first + count], MULT)
 
         x_codes = {}
-        x_planes = {}
+        x_bytes = {}
 
         def quantise(gated, a, first, count, tag):
-            grouped = keep.tile([P, PACK * count], BF16, tag=tag, name="grouped", align_bytes=64)
+            grouped = keep.tile([P, PACK * count], BF16, tag=tag, name="grouped", align_bytes=ALIGN)
             nc.scalar.copy(
                 out=grouped[:].rearrange("p (c i t) -> p c t i", i=LINE, t=PACK),
                 in_=gated.rearrange("p t (c i) -> p c t i", i=LINE),
             )
-            codes = keep.tile([P, count], U32, name="x_codes_%d_%d" % (a, first), align_bytes=64)
-            plane = keep.tile([P, count], U8, name="x_plane_%d_%d" % (a, first), align_bytes=64)
-            nc.vector.quantize_mx(out=codes[:].bitcast(FP8X4), scales=plane[:], in_=grouped[:])
+            codes = keep.tile([P, count], U32, name="x_codes_%d_%d" % (a, first), align_bytes=ALIGN)
+            scale_bytes = keep.tile([P, count], U8, name="x_bytes_%d_%d" % (a, first), align_bytes=ALIGN)
+            nc.vector.quantize_mx(out=codes[:].bitcast(FP8X4), scales=scale_bytes[:], in_=grouped[:])
             for at in range(0, count, C):
                 x_codes[a, (first + at) // C] = codes[:, at : at + C]
-                x_planes[a, (first + at) // C] = plane[:, at : at + C]
+                x_bytes[a, (first + at) // C] = scale_bytes[:, at : at + C]
 
         for a in range(LAST):
             gated = keep.tile([P, PACK, T], F32, name="gated_%d" % a)
@@ -109,16 +118,13 @@ def tile_moe_pre_lin_bias_kernel(tc, xT, w_words, w_scales, b, gate, offs, out):
             for first, count in ((0, 2 * PAIR), (2 * PAIR, PAIR)):
                 quantise(gated[:, :, first : first + count], a, first, count, "grouped_%d_%d" % (a, first))
 
-        def last_pass(pair):
-            tag = "last_grouped_0" if pair == 2 else "last_gated_%d" % pair
-            gated = keep.tile([P, PACK, PAIR], F32, tag=tag, name="gated", align_bytes=64)
+        def last_pass(pair, gated):
             for t in range(PACK):
                 gather(gated[:, t, :], LAST, t, pair * PAIR, PAIR)
-            quantise(gated[:], LAST, pair * PAIR, PAIR, "last_grouped_%d" % pair if pair < 2 else "grouped_end")
+            quantise(gated, LAST, pair * PAIR, PAIR, "end_%d" % pair)
 
-        def products(pair):
-            tag = "last_grouped_0" if pair == 1 else "by_expert_%d" % pair
-            by_expert = keep.tile([P, PAIR], F32, tag=tag, name="by_expert", align_bytes=64)
+        def products(pair, tag):
+            y = keep.tile([P, PAIR], F32, tag=tag, name="y", align_bytes=ALIGN)
             for j in range(2):
                 e = 2 * pair + j
                 acc = sums.tile([P, C], F32, name="acc")
@@ -127,23 +133,24 @@ def tile_moe_pre_lin_bias_kernel(tc, xT, w_words, w_scales, b, gate, offs, out):
                     nc.tensor.matmul_mx(
                         out=acc[:],
                         lhsT=w_codes[:, g * 2 * N : (g + 1) * 2 * N].bitcast(FP4X4),
-                        lhsT_scale=w_plane[:, g * N : (g + 1) * N],
+                        lhsT_scale=w_bytes[:, g * N : (g + 1) * N],
                         rhs=x_codes[a, e].bitcast(FP8X4),
-                        rhs_scale=x_planes[a, e],
+                        rhs_scale=x_bytes[a, e],
                         start=(a == 0),
                         stop=(a == LAST),
                     )
-                nc.scalar.activation(
-                    out=by_expert[:, j * C : (j + 1) * C], in_=acc[:], func=IDENTITY, bias=bias[:, e : e + 1]
-                )
-            return by_expert
+                nc.scalar.activation(out=y[:, j * C : (j + 1) * C], in_=acc[:], func=IDENTITY, bias=bias[:, e : e + 1])
+            return y
 
-        last_pass(0)
-        last_pass(1)
-        ready = [products(0)]
-        last_pass(2)
-        ready += [products(1), products(2)]
-        result = keep.tile([P, T], F32, tag="last_grouped_1", name="result", align_bytes=64)
+        two_pairs = keep.tile([P, 2, PACK, PAIR], F32, tag="tokens_%d_%d" % early[-1], name="gated", align_bytes=ALIGN)
+        last_pass(0, two_pairs[:, 0, :, :])
+        last_pass(1, two_pairs[:, 1, :, :])
+        ys = [products(0, "y_0")]
+        third_pair = keep.tile([P, PACK, PAIR], F32, tag="end_0", name="gated", align_bytes=ALIGN)
+        last_pass(2, third_pair[:])
+        ys += [products(1, "end_0"), products(2, "y_2")]
+
+        result = keep.tile([P, T], F32, tag="end_1", name="result", align_bytes=ALIGN)
         for pair in range(PAIRS):
-            nc.vector.tensor_copy(result[:].indirect(offsets_of(pair * PAIR, PAIR)), ready[pair][:])
+            nc.vector.tensor_copy(result[:].indirect(offsets_of(pair * PAIR, PAIR)), ys[pair][:])
         nc.sync.dma_start(out=out, in_=result[:])

from contextlib import ExitStack

import concourse.mybir as mybir

K, T, E, C, N = 2048, 768, 6, 128, 128

F32 = mybir.dt.float32
BF16 = mybir.dt.bfloat16
I32 = mybir.dt.int32
U32 = mybir.dt.uint32
U16 = mybir.dt.uint16
U8 = mybir.dt.uint8
FP8X4 = mybir.dt.float8_e4m3fn_x4
FP4X4 = mybir.dt.float4_e2m1fn_x4
IDENTITY = mybir.ActivationFunctionType.Identity
MULT = mybir.AluOpType.mult

P = 128
PACK = 4
PASSES = K // (P * PACK)
LAST = PASSES - 1
PAIR = 2 * C
PAIRS = E // 2
PER_COLUMN = 16
SPARE = 16
LINE = 4
QUADRANT = 32
SCALE_ROWS = 4
ALIGN = 64

FLOPS = 2 * K * N * E * C
BYTES = 4 * K * T + E * K * N // 2 + E * K * N // 32 + 4 * N * E + 4 * T + 2 * P * T // PER_COLUMN + 4 * N * T


def tile_moe_pre_lin_bias_kernel(tc, xT, w_words, w_scales, b, gate, offs, out):
    nc = tc.nc
    with ExitStack() as ctx:
        keep = ctx.enter_context(tc.tile_pool(name="keep", bufs=1))
        sums = ctx.enter_context(tc.psum_pool(name="sums", bufs=E))

        def by_pairs(a, t):
            return a == LAST or (a, t) == (0, 0)

        matrices = E * PASSES
        w_codes = keep.tile([P, matrices * 2 * N], U8, name="w_codes", align_bytes=ALIGN)
        w_bytes = keep.tile([P, matrices * N], U8, name="w_bytes", align_bytes=ALIGN)
        bias = keep.tile([P, E], F32, name="bias")

        def load_weights():
            nc.sync.dma_start(
                out=w_codes[:].bitcast(I32).rearrange("p (g n) -> p g n", g=matrices),
                in_=w_words.rearrange("e a p n -> p (e a) n").bitcast(I32),
            )
            w_bytes_raw = w_bytes[:].bitcast(I32)
            nc.gpsimd.memset(w_bytes_raw, 0)
            scale_rows = w_scales.rearrange("e a (q r) n -> r q (e a) n", r=SCALE_ROWS).bitcast(I32)
            for r in range(SCALE_ROWS):
                nc.sync.dma_start(
                    out=w_bytes_raw[r:P:QUADRANT, :].rearrange("q (g n) -> q g n", g=matrices),
                    in_=scale_rows[r],
                )
            nc.sync.dma_start(out=bias[:], in_=b)

        offsets = keep.tile([P, T // PER_COLUMN], U16, name="offsets")
        gates = keep.tile([P, T], F32, name="gates")
        rows = xT.rearrange("(a p t) w -> a p t w", p=P, t=PACK)
        window = {}

        def load_plane(a, t):
            width = T if by_pairs(a, t) else T + SPARE
            window[a, t] = keep.tile([P, width], F32, tag="tokens_%d_%d" % (a, t), name="tokens", align_bytes=ALIGN)
            nc.sync.dma_start(out=window[a, t][:, 0:T], in_=rows[a, :, t, :])
            if width > T:
                nc.gpsimd.memset(window[a, t][:, T:], 0.0)

        load_plane(0, 0)
        nc.sync.dma_start(offsets[:], offs)
        for pair in range(PAIRS):
            slots = slice(pair * PAIR, (pair + 1) * PAIR)
            nc.sync.dma_start(out=gates[:, slots], in_=gate[0:P, slots])
        early = [(a, t) for a in range(LAST) for t in range(PACK)]
        for a, t in early[1:-1]:
            load_plane(a, t)
        load_weights()
        for t in range(PACK):
            load_plane(LAST, t)
        load_plane(*early[-1])

        def offsets_of(first, count):
            return offsets[:, first // PER_COLUMN : (first + count) // PER_COLUMN]

        def gather(into, a, t, first, count):
            looked_up = window[a, t][:].indirect(offsets_of(first, count))
            nc.vector.tensor_tensor(into, looked_up, gates[:, first : first + count], MULT)

        x_codes = {}
        x_bytes = {}

        def quantise(gated, a, first, count, tag):
            grouped = keep.tile([P, PACK * count], BF16, tag=tag, name="grouped", align_bytes=ALIGN)
            nc.scalar.copy(
                out=grouped[:].rearrange("p (c i t) -> p c t i", i=LINE, t=PACK),
                in_=gated.rearrange("p t (c i) -> p c t i", i=LINE),
            )
            codes = keep.tile([P, count], U32, name="x_codes_%d_%d" % (a, first), align_bytes=ALIGN)
            scale_bytes = keep.tile([P, count], U8, name="x_bytes_%d_%d" % (a, first), align_bytes=ALIGN)
            nc.vector.quantize_mx(out=codes[:].bitcast(FP8X4), scales=scale_bytes[:], in_=grouped[:])
            for at in range(0, count, C):
                x_codes[a, (first + at) // C] = codes[:, at : at + C]
                x_bytes[a, (first + at) // C] = scale_bytes[:, at : at + C]

        for a in range(LAST):
            gated = keep.tile([P, PACK, T], F32, name="gated_%d" % a)
            for t in range(PACK):
                count = PAIR if by_pairs(a, t) else T
                for first in range(0, T, count):
                    gather(gated[:, t, first : first + count], a, t, first, count)
            for first, count in ((0, 2 * PAIR), (2 * PAIR, PAIR)):
                quantise(gated[:, :, first : first + count], a, first, count, "grouped_%d_%d" % (a, first))

        def last_pass(pair, gated):
            for t in range(PACK):
                gather(gated[:, t, :], LAST, t, pair * PAIR, PAIR)
            quantise(gated, LAST, pair * PAIR, PAIR, "end_%d" % pair)

        def products(pair, tag):
            y = keep.tile([P, PAIR], F32, tag=tag, name="y", align_bytes=ALIGN)
            for j in range(2):
                e = 2 * pair + j
                acc = sums.tile([P, C], F32, name="acc")
                for a in range(PASSES):
                    g = e * PASSES + a
                    nc.tensor.matmul_mx(
                        out=acc[:],
                        lhsT=w_codes[:, g * 2 * N : (g + 1) * 2 * N].bitcast(FP4X4),
                        lhsT_scale=w_bytes[:, g * N : (g + 1) * N],
                        rhs=x_codes[a, e].bitcast(FP8X4),
                        rhs_scale=x_bytes[a, e],
                        start=(a == 0),
                        stop=(a == LAST),
                    )
                nc.scalar.activation(out=y[:, j * C : (j + 1) * C], in_=acc[:], func=IDENTITY, bias=bias[:, e : e + 1])
            return y

        two_pairs = keep.tile([P, 2, PACK, PAIR], F32, tag="tokens_%d_%d" % early[-1], name="gated", align_bytes=ALIGN)
        last_pass(0, two_pairs[:, 0, :, :])
        last_pass(1, two_pairs[:, 1, :, :])
        ys = [products(0, "y_0")]
        third_pair = keep.tile([P, PACK, PAIR], F32, tag="end_0", name="gated", align_bytes=ALIGN)
        last_pass(2, third_pair[:])
        ys += [products(1, "end_0"), products(2, "y_2")]

        result = keep.tile([P, T], F32, tag="end_1", name="result", align_bytes=ALIGN)
        for pair in range(PAIRS):
            nc.vector.tensor_copy(result[:].indirect(offsets_of(pair * PAIR, PAIR)), ys[pair][:])
        nc.sync.dma_start(out=out, in_=result[:])
